import numpy as np
import ml_dtypes


def mxq(x, axis, fmt="e4m3"):
    dtype, down = {"e4m3": (ml_dtypes.float8_e4m3fn, 7), "e5m2": (ml_dtypes.float8_e5m2, 14)}[fmt]
    v = np.moveaxis(np.asarray(x, np.float32).astype(ml_dtypes.bfloat16).astype(np.float64), axis, -1)
    blocks = v.reshape(v.shape[:-1] + (-1, 32))
    amax = np.abs(blocks).max(-1, keepdims=True)
    byte = np.maximum(np.where(amax > 0, np.frexp(amax)[1] - 1 + 127, 0) - down, 1)
    scale = np.exp2(byte - 127.0)
    codes = (blocks / scale).astype(np.float32).astype(dtype).astype(np.float64)
    return np.moveaxis((codes * scale).reshape(v.shape), -1, axis)


WIDE = False


def mx_kscale(k):
    if not WIDE:
        return np.ones(k)
    levels = np.array([10, -10, 5, -5, 0])
    if k % 512:
        return np.exp2(np.random.permutation(np.resize(levels, k // 32))).repeat(32)
    a = np.empty((k // 512, 16))
    for p in range(k // 512):
        a[p, :8] = np.random.permutation(np.resize(levels, 8))
        for g in range(8):
            far = levels[np.abs(levels - a[p, g]) >= 10]
            a[p, g + 8] = far[np.random.randint(len(far))]
    return np.exp2(a.ravel()).repeat(32)


def f64(x):
    return np.asarray(x).astype(np.float64)


def striped(idx):
    return np.tile(idx.reshape(-1, 16).T, (8, 1)).astype(np.uint16)


def unstriped(offs):
    return offs[:16].T.reshape(-1).astype(np.int64)


def pack_weight(w):
    k, n = w.shape
    w = f64(np.asarray(w, np.float32).astype(ml_dtypes.bfloat16)).reshape(k // 32, 32, n)
    amax = np.abs(w).max(1)
    byte = np.clip(np.where(amax > 0, np.frexp(amax)[1] - 1 + 127 - 7, 1), 1, 254)
    scaled = (w * np.exp2(127.0 - byte)[:, None, :]).reshape(k, n).astype(np.float32)
    words = np.ascontiguousarray(scaled.reshape(k // 512, 128, 4, n).transpose(0, 1, 3, 2)).astype(ml_dtypes.float8_e4m3fn).view(np.uint8)
    return words, np.ascontiguousarray(byte.astype(np.uint8).reshape(k // 512, 16, n))


def unpack_weight(words, scales):
    g, p, n, _ = words.shape
    vals = np.ascontiguousarray(words).view(ml_dtypes.float8_e4m3fn).astype(np.float64) * np.repeat(np.exp2(scales.astype(np.float64) - 127.0), 8, axis=1)[..., None]
    return vals.transpose(0, 1, 3, 2).reshape(g * 512, n)


def relu(v):
    return np.maximum(v, 0.0)


K, T, S, D, H, N = 1024, 2048, 512, 8, 512, 256


def setup_inputs():
    n = np.random.standard_normal
    s = mx_kscale(K)[:, None]
    u = mx_kscale(H)
    packed_xT = pack_weight(n((K, T)) * s)
    return {
        "x_words": packed_xT[0],
        "x_scales": packed_xT[1],
        "w1": (n((K, H)) / np.sqrt(K) / s * u).astype(np.float32),
        "w2": (n((H, N)) / np.sqrt(H) / u[:, None]).astype(np.float32),
        "w3": (n((K, N)) / np.sqrt(K) / s).astype(np.float32),
        "offs": striped(np.random.permutation(T)[:S]),
    }


def reference(x_words, x_scales, w1, w2, w3, offs):
    xq = unpack_weight(x_words, x_scales)[:, unstriped(offs)]
    h = relu(mxq(f64(w1), 0, "e4m3").T @ xq)
    hf = mxq(f64(w2), 0, "e4m3").T @ mxq(h, 0, "e4m3")
    y = mxq(f64(w3), 0, "e4m3").T @ xq
    hl = hf * y
    mh = hf.reshape(len(hf), -1, D).mean(axis=2)
    ml = y.reshape(len(y), -1, D).mean(axis=2)
    co = hl.reshape(len(hl), -1, D).mean(axis=2) - (mh * ml)
    l2 = (y) ** 2
    va = l2.reshape(len(l2), -1, D).mean(axis=2) - ((ml) ** 2) + 0.1
    return ((co) ** 2) / va

@@ -1,0 +1,205 @@
+from contextlib import ExitStack
+
+import concourse.mybir as mybir
+from concourse.masks import make_identity
+
+K, T, S, D, H, N = 1024, 2048, 512, 8, 512, 256
+FLOPS = 2 * S * (K * H + H * N + K * N)
+
+F32 = mybir.dt.float32
+BF16 = mybir.dt.bfloat16
+I32 = mybir.dt.int32
+U32 = mybir.dt.uint32
+U16 = mybir.dt.uint16
+U8 = mybir.dt.uint8
+FP8X4 = mybir.dt.float8_e4m3fn_x4
+ACT = mybir.ActivationFunctionType
+ALU = mybir.AluOpType
+AX = mybir.AxisListType
+
+P = 128
+PACK = 4
+K_PASS = P * PACK
+PASSES = K // K_PASS
+M_TILES = N // P
+CHUNK = 128
+CHUNKS = S // CHUNK
+GROUPS = S // D
+LIST_COL = 16
+
+
+def tile_picked_ycvar_expl_p_kernel(tc, x_words, x_scales, w1, w2, w3, offs, out):
+    nc = tc.nc
+    with ExitStack() as ctx:
+        keep = ctx.enter_context(tc.tile_pool(name="keep", bufs=1))
+        psum = ctx.enter_context(tc.psum_pool(name="psum", bufs=1))
+
+        def sb(name, shape, dtype):
+            return keep.tile(shape, dtype, name=name, align_bytes=64)
+
+        offsets = keep.tile([P, S // LIST_COL], U16, name="offsets")
+        x_table = [sb("x_table%d" % o, [P, T], I32) for o in range(PASSES)]
+        s_table = sb("s_table", [P, T], U8)
+        raw_cols = PACK * H
+        sq_at = raw_cols - GROUPS
+        raw1_at = sq_at + 2 * S - GROUPS
+        shared = sb("shared", [P, raw1_at + raw_cols], F32)
+        y_sq = shared[:, sq_at : sq_at + 2 * S].rearrange("p (d u m v) -> p d u m v", d=D, u=2, m=M_TILES)
+        w1_raw = [shared[:, at : at + raw_cols].rearrange("p (j c) -> p j c", j=PACK) for at in (0, raw1_at)]
+        w3_raw = [sb("w3_raw%d" % o, [P, PACK, N], F32) for o in range(PASSES)]
+        w2_raw = sb("w2_raw", [P, PACK, N], F32)
+
+        def rows(w, o):
+            return w[o * K_PASS : (o + 1) * K_PASS, :].rearrange("(p j) c -> p j c", j=PACK)
+
+        def load_x(o):
+            nc.sync.dma_start(x_table[o][:], x_words[o].rearrange("p n t -> p (n t)").bitcast(I32))
+
+        nc.vector.memset(s_table[:].bitcast(I32), 0)
+        warm = sb("warm", [P, 2], F32)
+        nc.vector.memset(warm[:, 0:1], 1.0)
+        nc.scalar.activation(warm[:, 1:2], warm[:, 0:1], ACT.Abs_reciprocal_sqrt)
+        ident = sb("ident", [P, P], F32)
+        make_identity(nc, ident[:])
+
+        nc.sync.dma_start(w3_raw[0][:], rows(w3, 0))
+        nc.sync.dma_start(offsets[:], offs)
+        nc.sync.dma_start(w3_raw[1][:], rows(w3, 1))
+        for q in range(4):
+            nc.sync.dma_start(s_table[32 * q : 32 * q + 8, :].bitcast(I32), x_scales[:, 4 * q : 4 * q + 4, :].bitcast(I32))
+        load_x(0)
+        load_x(1)
+        for o in range(PASSES):
+            nc.sync.dma_start(w1_raw[o], rows(w1, o))
+        nc.sync.dma_start(w2_raw[:], rows(w2, 0))
+
+        def copy_on(engine, dst, src):
+            if engine == "vector":
+                nc.vector.tensor_copy(dst, src)
+            else:
+                nc.scalar.copy(dst, src)
+
+        def cast_plain(engine, grouped, raw, c0, c1):
+            dst = grouped[:].rearrange("p (c i j) -> p c j i", i=4, j=PACK)[:, c0 // 4 : c1 // 4]
+            src = raw[:].rearrange("p j (c i) -> p c j i", i=4)[:, c0 // 4 : c1 // 4]
+            copy_on(engine, dst, src)
+
+        def cast_dealt(engine, grouped, raw, t0, m0, m1):
+            dst = grouped[:].rearrange("p (t m j) -> p m j t", t=PACK, j=PACK)[:, m0:m1, :, t0 : t0 + 2]
+            src = raw.rearrange("p j (m t) -> p m j t", t=PACK)[:, m0:m1, :, t0 : t0 + 2]
+            copy_on(engine, dst, src)
+
+        def quantize(codes, scales, grouped, c0, c1):
+            nc.vector.quantize_mx(out=codes[:, c0:c1].bitcast(FP8X4), scales=scales[:, c0:c1], in_=grouped[:, PACK * c0 : PACK * c1])
+
+        def operand(name, width):
+            return sb(name + "_bf", [P, PACK * width], BF16), sb(name + "_codes", [P, width], U32), sb(name + "_scales", [P, width], U8)
+
+        w1_q = [operand("w1q%d" % o, H) for o in range(PASSES)]
+        w3_q = [operand("w3q%d" % o, N) for o in range(PASSES)]
+        w2_q = operand("w2q", N)
+        x_codes = [sb("x_codes%d" % o, [P, S], U32) for o in range(PASSES)]
+        x_bytes = sb("x_bytes", [P, S], U8)
+
+        def gather_words(o, j0, j1):
+            nc.vector.tensor_copy(x_codes[o][:, j0:j1], x_table[o][:].bitcast(U32).indirect(offsets[:, j0 // LIST_COL : j1 // LIST_COL]))
+
+        def mx(acc, stat, cols, rhs, rhs_scale, start, stop):
+            nc.tensor.matmul_mx(out=acc, lhsT=stat[1][:, cols].bitcast(FP8X4), lhsT_scale=stat[2][:, cols], rhs=rhs.bitcast(FP8X4), rhs_scale=rhs_scale, start=start, stop=stop)
+
+        half = S // 2
+        for o in range(PASSES):
+            cast_plain("scalar", w3_q[o][0], w3_raw[o], 0, 96)
+            cast_plain("vector", w3_q[o][0], w3_raw[o], 96, N)
+            quantize(w3_q[o][1], w3_q[o][2], w3_q[o][0], 0, N)
+        nc.vector.tensor_copy(x_bytes[:], s_table[:].indirect(offsets[:]))
+        gather_words(0, 0, S)
+        gather_words(1, 0, half)
+        gather_words(1, half, S)
+
+        gh = GROUPS // 2
+        mean_sq = sb("mean_sq", [P, 2, M_TILES * gh], F32)
+
+        def y_product(u):
+            cols = slice(u * half, (u + 1) * half)
+            banks = [psum.tile([P, half], F32, name="y_ps%d" % mt) for mt in range(M_TILES)]
+            for o in range(PASSES):
+                for mt in range(M_TILES):
+                    mx(banks[mt][:], w3_q[o], slice(mt * P, (mt + 1) * P), x_codes[o][:, cols], x_bytes[4 * o :, cols], o == 0, o == PASSES - 1)
+            return banks
+
+        def square(u, banks):
+            for mt in range(M_TILES):
+                nc.scalar.activation(y_sq[:, :, u, mt, :], banks[mt][:].rearrange("p (v d) -> p d v", d=D), ACT.Square)
+
+        def centre(u, banks, tag):
+            y_sum = sb(tag, [P, M_TILES, gh], F32)
+            y_cen = sb("y_cen%d" % u, [P, M_TILES, half], F32)
+            for mt in range(M_TILES):
+                nc.vector.tensor_reduce(y_sum[:, mt, :], banks[mt][:].rearrange("p (v d) -> p v d", d=D), AX.X, ALU.add)
+            for mt in range(M_TILES):
+                nc.vector.scalar_tensor_tensor(
+                    y_cen[:, mt, :].rearrange("p (v d) -> p v d", d=D),
+                    y_sum[:, mt, :].unsqueeze(2).to_broadcast([P, gh, D]),
+                    -1.0 / D,
+                    banks[mt][:].rearrange("p (v d) -> p v d", d=D),
+                    ALU.mult,
+                    ALU.add,
+                )
+            flat = y_sum[:].rearrange("p m v -> p (m v)")
+            nc.vector.scalar_tensor_tensor(mean_sq[:, u, :], flat, -1.0 / D, flat, ALU.mult, ALU.mult)
+            return y_cen
+
+        banks = y_product(0)
+        y_cen = [centre(0, banks, "y_sum0")]
+        cast_dealt("scalar", w1_q[0][0], w1_raw[0], 2, 0, P)
+        cast_dealt("vector", w1_q[0][0], w1_raw[0], 0, 0, P)
+        square(0, banks)
+        quantize(w1_q[0][1], w1_q[0][2], w1_q[0][0], 2 * P, 4 * P)
+        quantize(w1_q[0][1], w1_q[0][2], w1_q[0][0], 0, 2 * P)
+        banks = y_product(1)
+
+        cast_dealt("vector", w1_q[1][0], w1_raw[1], 0, 0, P)
+        cast_dealt("scalar", w1_q[1][0], w1_raw[1], 2, 0, 64)
+        cast_dealt("vector", w1_q[1][0], w1_raw[1], 2, 64, P)
+        quantize(w1_q[1][1], w1_q[1][2], w1_q[1][0], 0, 2 * P)
+        quantize(w1_q[1][1], w1_q[1][2], w1_q[1][0], 2 * P, 4 * P)
+        square(1, banks)
+        cast_plain("scalar", w2_q[0], w2_raw, 0, N)
+        quantize(w2_q[1], w2_q[2], w2_q[0], 0, N)
+
+        co_sum = sb("co_sum", [P, 2, M_TILES, gh], F32)
+        h_q = operand("hq", S)
+        for c in range(CHUNKS):
+            cols = slice(c * CHUNK, (c + 1) * CHUNK)
+            h_ps = psum.tile([P, PACK, CHUNK], F32, name="h_ps%d" % c)
+            for t in range(PACK):
+                for o in range(PASSES):
+                    mx(h_ps[:, t, :], w1_q[o], slice(t * P, (t + 1) * P), x_codes[o][:, cols], x_bytes[4 * o :, cols], o == 0, o == PASSES - 1)
+            nc.scalar.activation(h_q[0][:, PACK * c * CHUNK : PACK * (c + 1) * CHUNK].rearrange("p (j t) -> p j t", t=PACK), h_ps[:].rearrange("p t j -> p j t"), ACT.Relu)
+            quantize(h_q[1], h_q[2], h_q[0], c * CHUNK, (c + 1) * CHUNK)
+        y_cen.append(centre(1, banks, "w1q1_bf"))
+
+        for j0, j1, tag in [(c * CHUNK, (c + 1) * CHUNK, "hf_ps%d" % (c % 2)) for c in range(CHUNKS)]:
+            u, width = j0 // half, j1 - j0
+            hf_ps = psum.tile([P, M_TILES, width], F32, name=tag)
+            for mt in range(M_TILES):
+                mx(hf_ps[:, mt, :], w2_q, slice(mt * P, (mt + 1) * P), h_q[1][:, j0:j1], h_q[2][:, j0:j1], True, True)
+            prod = sb("prod%d" % j0, [P, M_TILES, width], F32)
+            nc.vector.tensor_tensor(prod[:], hf_ps[:], y_cen[u][:, :, j0 - u * half : j1 - u * half], ALU.mult)
+            nc.vector.tensor_reduce(co_sum[:, u, :, (j0 - u * half) // D : (j1 - u * half) // D], prod[:].rearrange("p m (v d) -> p m v d", d=D), AX.X, ALU.add)
+
+        sq_ps = psum.tile([P, P], F32, name="y_ps0")
+        for d in range(D):
+            nc.tensor.matmul(sq_ps[:], y_sq[:, d].rearrange("p u m v -> p (u m v)"), ident[:], start=(d == 0), stop=False, is_transpose=True)
+        nc.tensor.matmul(sq_ps[:], mean_sq[:].rearrange("p u w -> p (u w)"), ident[:], start=False, stop=True, is_transpose=True)
+        inv_t = sb("inv_t", [P, P], F32)
+        nc.scalar.activation(inv_t[:], sq_ps[:], ACT.Abs_reciprocal_sqrt, bias=0.1 * D * D, scale=float(D))
+        inv_ps = psum.tile([P, P], F32, name="y_ps1")
+        nc.tensor.transpose(inv_ps[:], inv_t[:], ident[:])
+
+        ratio = sb("ratio", [P, 2, M_TILES, gh], F32)
+        result = sb("result", [P, M_TILES, 2, gh], F32)
+        nc.vector.tensor_tensor(ratio[:].rearrange("p u m v -> p (u m v)"), inv_ps[:], co_sum[:].rearrange("p u m v -> p (u m v)"), ALU.mult)
+        nc.vector.tensor_tensor(result[:].rearrange("p m u v -> p u m v"), ratio[:], ratio[:], ALU.mult)
+        nc.sync.dma_start(out.rearrange("(m p) v -> p m v", p=P), result[:].rearrange("p m u v -> p m (u v)"))

@@ -59,15 +59,21 @@ def tile_picked_ycvar_expl_p_kernel(tc, x_words, x_scales, w1, w2, w3, offs, out
         warm = sb("warm", [P, 2], F32)
         nc.vector.memset(warm[:, 0:1], 1.0)
         nc.scalar.activation(warm[:, 1:2], warm[:, 0:1], ACT.Abs_reciprocal_sqrt)
+
         ident = sb("ident", [P, P], F32)
         make_identity(nc, ident[:])
 
-        nc.sync.dma_start(w3_raw[0][:], rows(w3, 0))
-        nc.sync.dma_start(offsets[:], offs)
-        nc.sync.dma_start(w3_raw[1][:], rows(w3, 1))
-        for q in range(4):
-            nc.sync.dma_start(s_table[32 * q : 32 * q + 8, :].bitcast(I32), x_scales[:, 4 * q : 4 * q + 4, :].bitcast(I32))
+        def load_scales(o):
+            for q in range(4):
+                at = 32 * q + 4 * o
+                nc.sync.dma_start(s_table[at : at + 4, :].bitcast(I32), x_scales[o, 4 * q : 4 * q + 4, :].bitcast(I32))
+
         load_x(0)
+        nc.sync.dma_start(offsets[:], offs)
+        load_scales(0)
+        for o in range(PASSES):
+            nc.sync.dma_start(w3_raw[o][:], rows(w3, o))
+        load_scales(1)
         load_x(1)
         for o in range(PASSES):
             nc.sync.dma_start(w1_raw[o], rows(w1, o))
@@ -108,12 +114,12 @@ def tile_picked_ycvar_expl_p_kernel(tc, x_words, x_scales, w1, w2, w3, offs, out
             nc.tensor.matmul_mx(out=acc, lhsT=stat[1][:, cols].bitcast(FP8X4), lhsT_scale=stat[2][:, cols], rhs=rhs.bitcast(FP8X4), rhs_scale=rhs_scale, start=start, stop=stop)
 
         half = S // 2
+        gather_words(0, 0, S)
         for o in range(PASSES):
             cast_plain("scalar", w3_q[o][0], w3_raw[o], 0, 96)
             cast_plain("vector", w3_q[o][0], w3_raw[o], 96, N)
             quantize(w3_q[o][1], w3_q[o][2], w3_q[o][0], 0, N)
         nc.vector.tensor_copy(x_bytes[:], s_table[:].indirect(offsets[:]))
-        gather_words(0, 0, S)
         gather_words(1, 0, half)
         gather_words(1, half, S)
 
@@ -123,8 +129,8 @@ def tile_picked_ycvar_expl_p_kernel(tc, x_words, x_scales, w1, w2, w3, offs, out
         def y_product(u):
             cols = slice(u * half, (u + 1) * half)
             banks = [psum.tile([P, half], F32, name="y_ps%d" % mt) for mt in range(M_TILES)]
-            for o in range(PASSES):
-                for mt in range(M_TILES):
+            for mt in range(M_TILES):
+                for o in range(PASSES):
                     mx(banks[mt][:], w3_q[o], slice(mt * P, (mt + 1) * P), x_codes[o][:, cols], x_bytes[4 * o :, cols], o == 0, o == PASSES - 1)
             return banks
 
@@ -152,11 +158,11 @@ def tile_picked_ycvar_expl_p_kernel(tc, x_words, x_scales, w1, w2, w3, offs, out
 
         banks = y_product(0)
         y_cen = [centre(0, banks, "y_sum0")]
-        cast_dealt("scalar", w1_q[0][0], w1_raw[0], 2, 0, P)
-        cast_dealt("vector", w1_q[0][0], w1_raw[0], 0, 0, P)
+        for t0 in (0, 2):
+            cast_dealt("scalar", w1_q[0][0], w1_raw[0], t0, 72, P)
+            cast_dealt("vector", w1_q[0][0], w1_raw[0], t0, 0, 72)
         square(0, banks)
-        quantize(w1_q[0][1], w1_q[0][2], w1_q[0][0], 2 * P, 4 * P)
-        quantize(w1_q[0][1], w1_q[0][2], w1_q[0][0], 0, 2 * P)
+        quantize(w1_q[0][1], w1_q[0][2], w1_q[0][0], 0, H)
         banks = y_product(1)
 
         cast_dealt("vector", w1_q[1][0], w1_raw[1], 0, 0, P)
@@ -170,17 +176,24 @@ def tile_picked_ycvar_expl_p_kernel(tc, x_words, x_scales, w1, w2, w3, offs, out
 
         co_sum = sb("co_sum", [P, 2, M_TILES, gh], F32)
         h_q = operand("hq", S)
+        edges = [c * CHUNK for c in range(CHUNKS)] + [S - CHUNK // 2, S]
+        pieces = list(zip(edges[:-1], edges[1:]))
         for c in range(CHUNKS):
             cols = slice(c * CHUNK, (c + 1) * CHUNK)
             h_ps = psum.tile([P, PACK, CHUNK], F32, name="h_ps%d" % c)
             for t in range(PACK):
                 for o in range(PASSES):
                     mx(h_ps[:, t, :], w1_q[o], slice(t * P, (t + 1) * P), x_codes[o][:, cols], x_bytes[4 * o :, cols], o == 0, o == PASSES - 1)
-            nc.scalar.activation(h_q[0][:, PACK * c * CHUNK : PACK * (c + 1) * CHUNK].rearrange("p (j t) -> p j t", t=PACK), h_ps[:].rearrange("p t j -> p j t"), ACT.Relu)
-            quantize(h_q[1], h_q[2], h_q[0], c * CHUNK, (c + 1) * CHUNK)
+            for j0, j1 in [piece for piece in pieces if piece[0] // CHUNK == c]:
+                nc.scalar.activation(
+                    h_q[0][:, PACK * j0 : PACK * j1].rearrange("p (j t) -> p j t", t=PACK),
+                    h_ps[:, :, j0 - c * CHUNK : j1 - c * CHUNK].rearrange("p t j -> p j t"),
+                    ACT.Relu,
+                )
+                quantize(h_q[1], h_q[2], h_q[0], j0, j1)
         y_cen.append(centre(1, banks, "w1q1_bf"))
 
-        for j0, j1, tag in [(c * CHUNK, (c + 1) * CHUNK, "hf_ps%d" % (c % 2)) for c in range(CHUNKS)]:
+        def covariance(j0, j1, tag):
             u, width = j0 // half, j1 - j0
             hf_ps = psum.tile([P, M_TILES, width], F32, name=tag)
             for mt in range(M_TILES):
@@ -189,14 +202,21 @@ def tile_picked_ycvar_expl_p_kernel(tc, x_words, x_scales, w1, w2, w3, offs, out
             nc.vector.tensor_tensor(prod[:], hf_ps[:], y_cen[u][:, :, j0 - u * half : j1 - u * half], ALU.mult)
             nc.vector.tensor_reduce(co_sum[:, u, :, (j0 - u * half) // D : (j1 - u * half) // D], prod[:].rearrange("p m (v d) -> p m v d", d=D), AX.X, ALU.add)
 
-        sq_ps = psum.tile([P, P], F32, name="y_ps0")
+        jobs = [piece + (tag,) for piece, tag in zip(pieces, ("hf_ps0", "y_ps0", "y_ps1", "h_ps0", "h_ps1"))]
+        for job in jobs[:2]:
+            covariance(*job)
+
+        sq_ps = psum.tile([P, P], F32, name="sq_ps")
         for d in range(D):
             nc.tensor.matmul(sq_ps[:], y_sq[:, d].rearrange("p u m v -> p (u m v)"), ident[:], start=(d == 0), stop=False, is_transpose=True)
         nc.tensor.matmul(sq_ps[:], mean_sq[:].rearrange("p u w -> p (u w)"), ident[:], start=False, stop=True, is_transpose=True)
         inv_t = sb("inv_t", [P, P], F32)
         nc.scalar.activation(inv_t[:], sq_ps[:], ACT.Abs_reciprocal_sqrt, bias=0.1 * D * D, scale=float(D))
-        inv_ps = psum.tile([P, P], F32, name="y_ps1")
+        inv_ps = psum.tile([P, P], F32, name="h_ps2")
         nc.tensor.transpose(inv_ps[:], inv_t[:], ident[:])
+
+        for job in jobs[2:]:
+            covariance(*job)
 
         ratio = sb("ratio", [P, 2, M_TILES, gh], F32)
         result = sb("result", [P, M_TILES, 2, gh], F32)

@@ -63,17 +63,12 @@ def tile_picked_ycvar_expl_p_kernel(tc, x_words, x_scales, w1, w2, w3, offs, out
         ident = sb("ident", [P, P], F32)
         make_identity(nc, ident[:])
 
-        def load_scales(o):
-            for q in range(4):
-                at = 32 * q + 4 * o
-                nc.sync.dma_start(s_table[at : at + 4, :].bitcast(I32), x_scales[o, 4 * q : 4 * q + 4, :].bitcast(I32))
-
         load_x(0)
         nc.sync.dma_start(offsets[:], offs)
-        load_scales(0)
+        for q in range(4):
+            nc.sync.dma_start(s_table[32 * q : 32 * q + 8, :].bitcast(I32), x_scales[:, 4 * q : 4 * q + 4, :].bitcast(I32))
         for o in range(PASSES):
             nc.sync.dma_start(w3_raw[o][:], rows(w3, o))
-        load_scales(1)
         load_x(1)
         for o in range(PASSES):
             nc.sync.dma_start(w1_raw[o], rows(w1, o))
@@ -115,11 +110,11 @@ def tile_picked_ycvar_expl_p_kernel(tc, x_words, x_scales, w1, w2, w3, offs, out
 
         half = S // 2
         gather_words(0, 0, S)
+        nc.vector.tensor_copy(x_bytes[:], s_table[:].indirect(offsets[:]))
         for o in range(PASSES):
             cast_plain("scalar", w3_q[o][0], w3_raw[o], 0, 96)
             cast_plain("vector", w3_q[o][0], w3_raw[o], 96, N)
             quantize(w3_q[o][1], w3_q[o][2], w3_q[o][0], 0, N)
-        nc.vector.tensor_copy(x_bytes[:], s_table[:].indirect(offsets[:]))
         gather_words(1, 0, half)
         gather_words(1, half, S)
 

from contextlib import ExitStack

import concourse.mybir as mybir
from concourse.masks import make_identity

K, T, S, D, H, N = 1024, 2048, 512, 8, 512, 256
FLOPS = 2 * S * (K * H + H * N + K * N)

F32 = mybir.dt.float32
BF16 = mybir.dt.bfloat16
I32 = mybir.dt.int32
U32 = mybir.dt.uint32
U16 = mybir.dt.uint16
U8 = mybir.dt.uint8
FP8X4 = mybir.dt.float8_e4m3fn_x4
ACT = mybir.ActivationFunctionType
ALU = mybir.AluOpType
AX = mybir.AxisListType

P = 128
PACK = 4
K_PASS = P * PACK
PASSES = K // K_PASS
M_TILES = N // P
CHUNK = 128
CHUNKS = S // CHUNK
GROUPS = S // D
LIST_COL = 16


def tile_picked_ycvar_expl_p_kernel(tc, x_words, x_scales, w1, w2, w3, offs, out):
    nc = tc.nc
    with ExitStack() as ctx:
        keep = ctx.enter_context(tc.tile_pool(name="keep", bufs=1))
        psum = ctx.enter_context(tc.psum_pool(name="psum", bufs=1))

        def sb(name, shape, dtype):
            return keep.tile(shape, dtype, name=name, align_bytes=64)

        offsets = keep.tile([P, S // LIST_COL], U16, name="offsets")
        x_table = [sb("x_table%d" % o, [P, T], I32) for o in range(PASSES)]
        s_table = sb("s_table", [P, T], U8)
        raw_cols = PACK * H
        sq_at = raw_cols - GROUPS
        raw1_at = sq_at + 2 * S - GROUPS
        shared = sb("shared", [P, raw1_at + raw_cols], F32)
        y_sq = shared[:, sq_at : sq_at + 2 * S].rearrange("p (d u m v) -> p d u m v", d=D, u=2, m=M_TILES)
        w1_raw = [shared[:, at : at + raw_cols].rearrange("p (j c) -> p j c", j=PACK) for at in (0, raw1_at)]
        w3_raw = [sb("w3_raw%d" % o, [P, PACK, N], F32) for o in range(PASSES)]
        w2_raw = sb("w2_raw", [P, PACK, N], F32)

        def rows(w, o):
            return w[o * K_PASS : (o + 1) * K_PASS, :].rearrange("(p j) c -> p j c", j=PACK)

        def load_x(o):
            nc.sync.dma_start(x_table[o][:], x_words[o].rearrange("p n t -> p (n t)").bitcast(I32))

        nc.vector.memset(s_table[:].bitcast(I32), 0)
        warm = sb("warm", [P, 2], F32)
        nc.vector.memset(warm[:, 0:1], 1.0)
        nc.scalar.activation(warm[:, 1:2], warm[:, 0:1], ACT.Abs_reciprocal_sqrt)

        ident = sb("ident", [P, P], F32)
        make_identity(nc, ident[:])

        load_x(0)
        nc.sync.dma_start(offsets[:], offs)
        for q in range(4):
            nc.sync.dma_start(s_table[32 * q : 32 * q + 8, :].bitcast(I32), x_scales[:, 4 * q : 4 * q + 4, :].bitcast(I32))
        for o in range(PASSES):
            nc.sync.dma_start(w3_raw[o][:], rows(w3, o))
        load_x(1)
        for o in range(PASSES):
            nc.sync.dma_start(w1_raw[o], rows(w1, o))
        nc.sync.dma_start(w2_raw[:], rows(w2, 0))

        def copy_on(engine, dst, src):
            if engine == "vector":
                nc.vector.tensor_copy(dst, src)
            else:
                nc.scalar.copy(dst, src)

        def cast_plain(engine, grouped, raw, c0, c1):
            dst = grouped[:].rearrange("p (c i j) -> p c j i", i=4, j=PACK)[:, c0 // 4 : c1 // 4]
            src = raw[:].rearrange("p j (c i) -> p c j i", i=4)[:, c0 // 4 : c1 // 4]
            copy_on(engine, dst, src)

        def cast_dealt(engine, grouped, raw, t0, m0, m1):
            dst = grouped[:].rearrange("p (t m j) -> p m j t", t=PACK, j=PACK)[:, m0:m1, :, t0 : t0 + 2]
            src = raw.rearrange("p j (m t) -> p m j t", t=PACK)[:, m0:m1, :, t0 : t0 + 2]
            copy_on(engine, dst, src)

        def quantize(codes, scales, grouped, c0, c1):
            nc.vector.quantize_mx(out=codes[:, c0:c1].bitcast(FP8X4), scales=scales[:, c0:c1], in_=grouped[:, PACK * c0 : PACK * c1])

        def operand(name, width):
            return sb(name + "_bf", [P, PACK * width], BF16), sb(name + "_codes", [P, width], U32), sb(name + "_scales", [P, width], U8)

        w1_q = [operand("w1q%d" % o, H) for o in range(PASSES)]
        w3_q = [operand("w3q%d" % o, N) for o in range(PASSES)]
        w2_q = operand("w2q", N)
        x_codes = [sb("x_codes%d" % o, [P, S], U32) for o in range(PASSES)]
        x_bytes = sb("x_bytes", [P, S], U8)

        def gather_words(o, j0, j1):
            nc.vector.tensor_copy(x_codes[o][:, j0:j1], x_table[o][:].bitcast(U32).indirect(offsets[:, j0 // LIST_COL : j1 // LIST_COL]))

        def mx(acc, stat, cols, rhs, rhs_scale, start, stop):
            nc.tensor.matmul_mx(out=acc, lhsT=stat[1][:, cols].bitcast(FP8X4), lhsT_scale=stat[2][:, cols], rhs=rhs.bitcast(FP8X4), rhs_scale=rhs_scale, start=start, stop=stop)

        half = S // 2
        gather_words(0, 0, S)
        nc.vector.tensor_copy(x_bytes[:], s_table[:].indirect(offsets[:]))
        for o in range(PASSES):
            cast_plain("scalar", w3_q[o][0], w3_raw[o], 0, 96)
            cast_plain("vector", w3_q[o][0], w3_raw[o], 96, N)
            quantize(w3_q[o][1], w3_q[o][2], w3_q[o][0], 0, N)
        gather_words(1, 0, half)
        gather_words(1, half, S)

        gh = GROUPS // 2
        mean_sq = sb("mean_sq", [P, 2, M_TILES * gh], F32)

        def y_product(u):
            cols = slice(u * half, (u + 1) * half)
            banks = [psum.tile([P, half], F32, name="y_ps%d" % mt) for mt in range(M_TILES)]
            for mt in range(M_TILES):
                for o in range(PASSES):
                    mx(banks[mt][:], w3_q[o], slice(mt * P, (mt + 1) * P), x_codes[o][:, cols], x_bytes[4 * o :, cols], o == 0, o == PASSES - 1)
            return banks

        def square(u, banks):
            for mt in range(M_TILES):
                nc.scalar.activation(y_sq[:, :, u, mt, :], banks[mt][:].rearrange("p (v d) -> p d v", d=D), ACT.Square)

        def centre(u, banks, tag):
            y_sum = sb(tag, [P, M_TILES, gh], F32)
            y_cen = sb("y_cen%d" % u, [P, M_TILES, half], F32)
            for mt in range(M_TILES):
                nc.vector.tensor_reduce(y_sum[:, mt, :], banks[mt][:].rearrange("p (v d) -> p v d", d=D), AX.X, ALU.add)
            for mt in range(M_TILES):
                nc.vector.scalar_tensor_tensor(
                    y_cen[:, mt, :].rearrange("p (v d) -> p v d", d=D),
                    y_sum[:, mt, :].unsqueeze(2).to_broadcast([P, gh, D]),
                    -1.0 / D,
                    banks[mt][:].rearrange("p (v d) -> p v d", d=D),
                    ALU.mult,
                    ALU.add,
                )
            flat = y_sum[:].rearrange("p m v -> p (m v)")
            nc.vector.scalar_tensor_tensor(mean_sq[:, u, :], flat, -1.0 / D, flat, ALU.mult, ALU.mult)
            return y_cen

        banks = y_product(0)
        y_cen = [centre(0, banks, "y_sum0")]
        for t0 in (0, 2):
            cast_dealt("scalar", w1_q[0][0], w1_raw[0], t0, 72, P)
            cast_dealt("vector", w1_q[0][0], w1_raw[0], t0, 0, 72)
        square(0, banks)
        quantize(w1_q[0][1], w1_q[0][2], w1_q[0][0], 0, H)
        banks = y_product(1)

        cast_dealt("vector", w1_q[1][0], w1_raw[1], 0, 0, P)
        cast_dealt("scalar", w1_q[1][0], w1_raw[1], 2, 0, 64)
        cast_dealt("vector", w1_q[1][0], w1_raw[1], 2, 64, P)
        quantize(w1_q[1][1], w1_q[1][2], w1_q[1][0], 0, 2 * P)
        quantize(w1_q[1][1], w1_q[1][2], w1_q[1][0], 2 * P, 4 * P)
        square(1, banks)
        cast_plain("scalar", w2_q[0], w2_raw, 0, N)
        quantize(w2_q[1], w2_q[2], w2_q[0], 0, N)

        co_sum = sb("co_sum", [P, 2, M_TILES, gh], F32)
        h_q = operand("hq", S)
        edges = [c * CHUNK for c in range(CHUNKS)] + [S - CHUNK // 2, S]
        pieces = list(zip(edges[:-1], edges[1:]))
        for c in range(CHUNKS):
            cols = slice(c * CHUNK, (c + 1) * CHUNK)
            h_ps = psum.tile([P, PACK, CHUNK], F32, name="h_ps%d" % c)
            for t in range(PACK):
                for o in range(PASSES):
                    mx(h_ps[:, t, :], w1_q[o], slice(t * P, (t + 1) * P), x_codes[o][:, cols], x_bytes[4 * o :, cols], o == 0, o == PASSES - 1)
            for j0, j1 in [piece for piece in pieces if piece[0] // CHUNK == c]:
                nc.scalar.activation(
                    h_q[0][:, PACK * j0 : PACK * j1].rearrange("p (j t) -> p j t", t=PACK),
                    h_ps[:, :, j0 - c * CHUNK : j1 - c * CHUNK].rearrange("p t j -> p j t"),
                    ACT.Relu,
                )
                quantize(h_q[1], h_q[2], h_q[0], j0, j1)
        y_cen.append(centre(1, banks, "w1q1_bf"))

        def covariance(j0, j1, tag):
            u, width = j0 // half, j1 - j0
            hf_ps = psum.tile([P, M_TILES, width], F32, name=tag)
            for mt in range(M_TILES):
                mx(hf_ps[:, mt, :], w2_q, slice(mt * P, (mt + 1) * P), h_q[1][:, j0:j1], h_q[2][:, j0:j1], True, True)
            prod = sb("prod%d" % j0, [P, M_TILES, width], F32)
            nc.vector.tensor_tensor(prod[:], hf_ps[:], y_cen[u][:, :, j0 - u * half : j1 - u * half], ALU.mult)
            nc.vector.tensor_reduce(co_sum[:, u, :, (j0 - u * half) // D : (j1 - u * half) // D], prod[:].rearrange("p m (v d) -> p m v d", d=D), AX.X, ALU.add)

        jobs = [piece + (tag,) for piece, tag in zip(pieces, ("hf_ps0", "y_ps0", "y_ps1", "h_ps0", "h_ps1"))]
        for job in jobs[:2]:
            covariance(*job)

        sq_ps = psum.tile([P, P], F32, name="sq_ps")
        for d in range(D):
            nc.tensor.matmul(sq_ps[:], y_sq[:, d].rearrange("p u m v -> p (u m v)"), ident[:], start=(d == 0), stop=False, is_transpose=True)
        nc.tensor.matmul(sq_ps[:], mean_sq[:].rearrange("p u w -> p (u w)"), ident[:], start=False, stop=True, is_transpose=True)
        inv_t = sb("inv_t", [P, P], F32)
        nc.scalar.activation(inv_t[:], sq_ps[:], ACT.Abs_reciprocal_sqrt, bias=0.1 * D * D, scale=float(D))
        inv_ps = psum.tile([P, P], F32, name="h_ps2")
        nc.tensor.transpose(inv_ps[:], inv_t[:], ident[:])

        for job in jobs[2:]:
            covariance(*job)

        ratio = sb("ratio", [P, 2, M_TILES, gh], F32)
        result = sb("result", [P, M_TILES, 2, gh], F32)
        nc.vector.tensor_tensor(ratio[:].rearrange("p u m v -> p (u m v)"), inv_ps[:], co_sum[:].rearrange("p u m v -> p (u m v)"), ALU.mult)
        nc.vector.tensor_tensor(result[:].rearrange("p m u v -> p u m v"), ratio[:], ratio[:], ALU.mult)
        nc.sync.dma_start(out.rearrange("(m p) v -> p m v", p=P), result[:].rearrange("p m u v -> p m (u v)"))
